import numpy as np
import ml_dtypes


def mxq(x, axis, fmt="e4m3"):
    dtype, down = {"e4m3": (ml_dtypes.float8_e4m3fn, 7), "e5m2": (ml_dtypes.float8_e5m2, 14)}[fmt]
    v = np.moveaxis(np.asarray(x, np.float32).astype(ml_dtypes.bfloat16).astype(np.float64), axis, -1)
    blocks = v.reshape(v.shape[:-1] + (-1, 32))
    amax = np.abs(blocks).max(-1, keepdims=True)
    byte = np.maximum(np.where(amax > 0, np.frexp(amax)[1] - 1 + 127, 0) - down, 1)
    scale = np.exp2(byte - 127.0)
    codes = (blocks / scale).astype(np.float32).astype(dtype).astype(np.float64)
    return np.moveaxis((codes * scale).reshape(v.shape), -1, axis)


WIDE = False


def mx_kscale(k):
    if not WIDE:
        return np.ones(k)
    levels = np.array([30, -30])
    if k % 512:
        return np.exp2(np.random.permutation(np.resize(levels, k // 32))).repeat(32)
    a = np.empty((k // 512, 16))
    for p in range(k // 512):
        a[p, :8] = np.random.permutation(np.resize(levels, 8))
        for g in range(8):
            far = levels[np.abs(levels - a[p, g]) >= 10]
            a[p, g + 8] = far[np.random.randint(len(far))]
    return np.exp2(a.ravel()).repeat(32)


def f64(x):
    return np.asarray(x).astype(np.float64)


def striped(idx):
    return np.tile(np.asarray(idx).reshape(-1, 16).T, (8, 1)).astype(np.uint16)


def unstriped(offs):
    return offs[:16].T.reshape(-1).astype(np.int64)


E2M1 = np.array([0.0, 0.5, 1.0, 1.5, 2.0, 3.0, 4.0, 6.0, -0.0, -0.5, -1.0, -1.5, -2.0, -3.0, -4.0, -6.0])


def pack_weight(w, fmt):
    k, n = w.shape
    w = f64(np.asarray(w, np.float32).astype(ml_dtypes.bfloat16)).reshape(k // 32, 32, n)
    amax = np.abs(w).max(1)
    if fmt == "e4m3":
        byte = np.frexp(amax)[1] - 1 + 127 - 7
    else:
        mant, ex = np.frexp(amax / 6.0)
        byte = np.where(mant > 0.5, ex, ex - 1) + 127
    byte = np.clip(np.where(amax > 0, byte, 1), 1, 254)
    scaled = (w * np.exp2(127.0 - byte)[:, None, :]).reshape(k, n).astype(np.float32)
    by_word = np.ascontiguousarray(scaled.reshape(k // 512, 128, 4, n).transpose(0, 1, 3, 2))
    if fmt == "e4m3":
        words = by_word.astype(ml_dtypes.float8_e4m3fn).view(np.uint8)
    else:
        c = by_word.astype(ml_dtypes.float4_e2m1fn).view(np.uint8) & 0xF
        words = (c[..., 0::2] | (c[..., 1::2] << 4)).reshape(k // 512, 128, 2 * n)
    return np.ascontiguousarray(words), np.ascontiguousarray(byte.astype(np.uint8).reshape(k // 512, 16, n))


def unpack_weight(words, scales, fmt):
    g, _, n = scales.shape
    words = np.ascontiguousarray(words).reshape(g, 128, n, -1)
    if fmt == "e4m3":
        vals = words.view(ml_dtypes.float8_e4m3fn).astype(np.float64)
    else:
        nib = np.empty((g, 128, n, 4), np.uint8)
        nib[..., 0::2] = words & 0xF
        nib[..., 1::2] = words >> 4
        vals = E2M1[nib]
    vals = vals * np.repeat(np.exp2(scales.astype(np.float64) - 127.0), 8, axis=1)[..., None]
    return vals.transpose(0, 1, 3, 2).reshape(g * 512, n)


N, K, T, J, B = 1024, 512, 2048, 512, 64


def setup_inputs():
    n = np.random.standard_normal
    idx = np.random.permutation(T)[:J]
    fn = mx_kscale(N)
    wp = pack_weight(n((N, K)) * 1 / np.sqrt(N) * fn[:, None], "e2m1")
    return {
        "g": (n((N, T)) * np.exp(0.5 * n((1, T))) / fn[:, None]).astype(np.float32),
        "w_words": wp[0],
        "w_scales": wp[1],
        "rw": (np.random.uniform(0.5, 2.0, (1, J))).astype(np.float32),
        "offs": striped(idx),
    }


def reference(g, w_words, w_scales, rw, offs):
    idx = unstriped(offs)
    wu = unpack_weight(w_words, w_scales, "e2m1")
    m = f64(g)[:, idx].reshape(N, B, J // B).mean(axis=2)
    mr = np.repeat(m, J // B, axis=1)
    d = f64(g)[:, idx] - mr
    dq = mxq(d, 0, "e5m2")
    dx = wu.T @ dq
    y = dx * f64(rw)
    return y

@@ -1,0 +1,135 @@
+from contextlib import ExitStack
+
+import concourse.mybir as mybir
+from concourse.masks import make_identity
+
+N, K, T, J = 1024, 512, 2048, 512
+FLOPS = 2 * N * K * J
+
+F32 = mybir.dt.float32
+BF16 = mybir.dt.bfloat16
+I32 = mybir.dt.int32
+U32 = mybir.dt.uint32
+U16 = mybir.dt.uint16
+U8 = mybir.dt.uint8
+E5M2X4 = mybir.dt.float8_e5m2_x4
+E2M1X4 = mybir.dt.float4_e2m1fn_x4
+ADD = mybir.AluOpType.add
+MULT = mybir.AluOpType.mult
+AXIS_X = mybir.AxisListType.X
+
+P = 128
+PACK = 4
+PASS_ROWS = P * PACK
+PASSES = N // PASS_ROWS
+GROUP = 8
+HALVES = 2
+HALF = J // HALVES
+LIST_ROWS = 16
+K_TILES = K // P
+
+
+def tile_list_group_relative_grad_kernel(tc, g, w_words, w_scales, rw, offs, out):
+    nc = tc.nc
+    planes = [(1, 2), (0, 0), (0, 1), (0, 2), (0, 3), (1, 0), (1, 1), (1, 3)]
+    g_planes = g.rearrange("(z p t) c -> z t p c", z=PASSES, t=PACK)
+
+    with ExitStack() as ctx:
+        keep = ctx.enter_context(tc.tile_pool(name="keep", bufs=1))
+        work = ctx.enter_context(tc.tile_pool(name="work", bufs=3))
+        psum = ctx.enter_context(tc.psum_pool(name="psum", bufs=1))
+
+        offsets = keep.tile([P, J // LIST_ROWS], U16, name="offsets")
+        windows = [keep.tile([P, T], F32, name="window%d" % i) for i in range(len(planes))]
+        words = keep.tile([P, PASSES, 2 * K], U8, name="words", align_bytes=64)
+        wscales = keep.tile([P, PASSES, K], U8, name="wscales", align_bytes=64)
+        rw_rows = keep.tile([P, J // P], F32, name="rw_rows")
+        rw_all = keep.tile([P, J], F32, name="rw_all")
+        ident = keep.tile([P, P], F32, name="ident")
+
+        nc.vector.memset(wscales[:].rearrange("p z c -> p (z c)").bitcast(I32), 0)
+        nc.scalar.dma_start(out=rw_rows[:], in_=rw.rearrange("o (p c) -> (o p) c", p=P))
+        for i, (z, t) in enumerate(planes):
+            nc.sync.dma_start(out=windows[i][:], in_=g_planes[z, t])
+            if i == 0:
+                nc.sync.dma_start(offsets[:], offs)
+        for q in range(4):
+            nc.sync.dma_start(
+                out=wscales[32 * q : 32 * q + 4].bitcast(I32),
+                in_=w_scales[:, 4 * q : 4 * q + 4, :].rearrange("z r c -> r z c").bitcast(I32),
+            )
+        nc.sync.dma_start(out=words[:].bitcast(I32), in_=w_words.rearrange("z p c -> p z c").bitcast(I32))
+
+        make_identity(nc, ident[:])
+        rw_bank = psum.tile([P, J // P, P], F32, name="rw_bank")
+        for c in range(J // P):
+            nc.tensor.transpose(rw_bank[:, c, :], rw_rows[:, c : c + 1].to_broadcast([P, P]), ident[:])
+        nc.scalar.copy(
+            out=rw_all[:].rearrange("p (n c) -> p n c", c=J // P),
+            in_=rw_bank[:].rearrange("p c n -> p n c"),
+        )
+
+        woven = [
+            [keep.tile([P, HALF, PACK], BF16, name="woven%d_%d" % (z, h), align_bytes=64) for h in range(HALVES)]
+            for z in range(PASSES)
+        ]
+        codes = [keep.tile([P, J], U32, name="codes%d" % z, align_bytes=64) for z in range(PASSES)]
+        dscales = [keep.tile([P, J], U8, name="dscales%d" % z, align_bytes=64) for z in range(PASSES)]
+        banks = [psum.tile([P, J], F32, name="bank%d" % m) for m in range(K_TILES)]
+
+        def by_group(ap):
+            return ap.rearrange("p (b i) -> p b i", i=GROUP)
+
+        def multiply(z):
+            for m in range(K_TILES):
+                nc.tensor.matmul_mx(
+                    out=banks[m][:],
+                    lhsT=words[:, z, 2 * P * m : 2 * P * (m + 1)].bitcast(E2M1X4),
+                    lhsT_scale=wscales[:, z, P * m : P * (m + 1)],
+                    rhs=codes[z][:].bitcast(E5M2X4),
+                    rhs_scale=dscales[z][:],
+                    start=(z == 0),
+                    stop=(z == PASSES - 1),
+                )
+
+        done = [0] * PASSES
+        for i, (z, t) in enumerate(planes):
+            last = i == len(planes) - 1
+            picked = [work.tile([P, HALF], F32, name="picked%d" % h) for h in range(HALVES)]
+            sums = [work.tile([P, HALF // GROUP], F32, name="sums%d" % h) for h in range(HALVES)]
+            cols = HALF // LIST_ROWS
+            for h in range(HALVES):
+                nc.vector.tensor_copy(picked[h][:], windows[i][:].indirect(offsets[:, h * cols : (h + 1) * cols]))
+            for h in range(HALVES):
+                nc.vector.tensor_reduce(sums[h][:], by_group(picked[h][:]), AXIS_X, ADD)
+            for h in range(HALVES):
+                direct = last and h == HALVES - 1
+                if direct:
+                    target = woven[z][h][:, :, t]
+                else:
+                    diff = work.tile([P, HALF], BF16, name="diff%d" % h)
+                    target = diff[:]
+                nc.vector.scalar_tensor_tensor(
+                    out=by_group(target),
+                    in0=sums[h][:].unsqueeze(2).to_broadcast([P, HALF // GROUP, GROUP]),
+                    scalar=-1.0 / GROUP,
+                    in1=by_group(picked[h][:]),
+                    op0=MULT,
+                    op1=ADD,
+                )
+                if not direct:
+                    nc.scalar.copy(out=woven[z][h][:, :, t], in_=diff[:])
+            done[z] = done[z] + 1
+            if done[z] == PACK:
+                for h in range(HALVES):
+                    nc.vector.quantize_mx(
+                        out=codes[z][:, h * HALF : (h + 1) * HALF].bitcast(E5M2X4),
+                        scales=dscales[z][:, h * HALF : (h + 1) * HALF],
+                        in_=woven[z][h][:].rearrange("p j t -> p (j t)"),
+                    )
+                multiply(z)
+
+        for m in range(K_TILES):
+            result = keep.tile([P, J], F32, name="result%d" % m)
+            nc.vector.tensor_tensor(result[:], banks[m][:], rw_all[:], MULT)
+            nc.sync.dma_start(out=out[P * m : P * (m + 1), :], in_=result[:])

@@ -16,6 +16,8 @@ E5M2X4 = mybir.dt.float8_e5m2_x4
 E2M1X4 = mybir.dt.float4_e2m1fn_x4
 ADD = mybir.AluOpType.add
 MULT = mybir.AluOpType.mult
+SUBTRACT = mybir.AluOpType.subtract
+COPY = mybir.ActivationFunctionType.Copy
 AXIS_X = mybir.AxisListType.X
 
 P = 128
@@ -31,7 +33,7 @@ K_TILES = K // P
 
 def tile_list_group_relative_grad_kernel(tc, g, w_words, w_scales, rw, offs, out):
     nc = tc.nc
-    planes = [(1, 2), (0, 0), (0, 1), (0, 2), (0, 3), (1, 0), (1, 1), (1, 3)]
+    planes = [(0, 0), (0, 1), (0, 2), (0, 3), (1, 2), (1, 0), (1, 1), (1, 3)]
     g_planes = g.rearrange("(z p t) c -> z t p c", z=PASSES, t=PACK)
 
     with ExitStack() as ctx:
@@ -40,7 +42,7 @@ def tile_list_group_relative_grad_kernel(tc, g, w_words, w_scales, rw, offs, out
         psum = ctx.enter_context(tc.psum_pool(name="psum", bufs=1))
 
         offsets = keep.tile([P, J // LIST_ROWS], U16, name="offsets")
-        windows = [keep.tile([P, T], F32, name="window%d" % i) for i in range(len(planes))]
+        windows = [keep.tile([P, T], F32, name="window%d" % i, align_bytes=64) for i in range(len(planes))]
         words = keep.tile([P, PASSES, 2 * K], U8, name="words", align_bytes=64)
         wscales = keep.tile([P, PASSES, K], U8, name="wscales", align_bytes=64)
         rw_rows = keep.tile([P, J // P], F32, name="rw_rows")
@@ -73,7 +75,7 @@ def tile_list_group_relative_grad_kernel(tc, g, w_words, w_scales, rw, offs, out
             [keep.tile([P, HALF, PACK], BF16, name="woven%d_%d" % (z, h), align_bytes=64) for h in range(HALVES)]
             for z in range(PASSES)
         ]
-        codes = [keep.tile([P, J], U32, name="codes%d" % z, align_bytes=64) for z in range(PASSES)]
+        codes = {}
         dscales = [keep.tile([P, J], U8, name="dscales%d" % z, align_bytes=64) for z in range(PASSES)]
         banks = [psum.tile([P, J], F32, name="bank%d" % m) for m in range(K_TILES)]
 
@@ -92,42 +94,67 @@ def tile_list_group_relative_grad_kernel(tc, g, w_words, w_scales, rw, offs, out
                     stop=(z == PASSES - 1),
                 )
 
-        done = [0] * PASSES
-        for i, (z, t) in enumerate(planes):
-            last = i == len(planes) - 1
-            picked = [work.tile([P, HALF], F32, name="picked%d" % h) for h in range(HALVES)]
-            sums = [work.tile([P, HALF // GROUP], F32, name="sums%d" % h) for h in range(HALVES)]
-            cols = HALF // LIST_ROWS
-            for h in range(HALVES):
-                nc.vector.tensor_copy(picked[h][:], windows[i][:].indirect(offsets[:, h * cols : (h + 1) * cols]))
-            for h in range(HALVES):
-                nc.vector.tensor_reduce(sums[h][:], by_group(picked[h][:]), AXIS_X, ADD)
-            for h in range(HALVES):
-                direct = last and h == HALVES - 1
-                if direct:
-                    target = woven[z][h][:, :, t]
-                else:
-                    diff = work.tile([P, HALF], BF16, name="diff%d" % h)
-                    target = diff[:]
-                nc.vector.scalar_tensor_tensor(
-                    out=by_group(target),
-                    in0=sums[h][:].unsqueeze(2).to_broadcast([P, HALF // GROUP, GROUP]),
-                    scalar=-1.0 / GROUP,
-                    in1=by_group(picked[h][:]),
-                    op0=MULT,
-                    op1=ADD,
+        picked = [keep.tile([P, J], F32, name="picked%d" % i) for i in range(len(planes))]
+        groups = HALF // GROUP
+
+        def spread(tile):
+            return tile[:].unsqueeze(2).to_broadcast([P, groups, GROUP])
+
+        def gather_and_sum(i, order, tags):
+            sums = {}
+            for h in order:
+                lo, hi = h * HALF, (h + 1) * HALF
+                nc.vector.tensor_copy(
+                    picked[i][:, lo:hi], windows[i][:].indirect(offsets[:, lo // LIST_ROWS : hi // LIST_ROWS])
                 )
-                if not direct:
-                    nc.scalar.copy(out=woven[z][h][:, :, t], in_=diff[:])
-            done[z] = done[z] + 1
-            if done[z] == PACK:
-                for h in range(HALVES):
-                    nc.vector.quantize_mx(
-                        out=codes[z][:, h * HALF : (h + 1) * HALF].bitcast(E5M2X4),
-                        scales=dscales[z][:, h * HALF : (h + 1) * HALF],
-                        in_=woven[z][h][:].rearrange("p j t -> p (j t)"),
-                    )
-                multiply(z)
+            for h in order:
+                sums[h] = keep.tile([P, groups], F32, name="sums%d_%d" % (i, h), tag=tags[h])
+                nc.vector.tensor_reduce(sums[h][:], by_group(picked[i][:, h * HALF : (h + 1) * HALF]), AXIS_X, ADD)
+            return sums
+
+        def subtract(i, h, sums, target):
+            nc.vector.scalar_tensor_tensor(
+                out=by_group(target),
+                in0=spread(sums[h]),
+                scalar=-1.0 / GROUP,
+                in1=by_group(picked[i][:, h * HALF : (h + 1) * HALF]),
+                op0=MULT,
+                op1=ADD,
+            )
+
+        def quantize(z, tag):
+            codes[z] = keep.tile([P, J], U32, name="codes%d" % z, tag=tag, align_bytes=64)
+            for h in range(HALVES):
+                nc.vector.quantize_mx(
+                    out=codes[z][:, h * HALF : (h + 1) * HALF].bitcast(E5M2X4),
+                    scales=dscales[z][:, h * HALF : (h + 1) * HALF],
+                    in_=woven[z][h][:].rearrange("p j t -> p (j t)"),
+                )
+
+        last = len(planes) - 1
+        for i in range(last):
+            z, t = planes[i]
+            sums = gather_and_sum(i, (1, 0), ["sums%d_%d" % (i, h) for h in range(HALVES)])
+            for h in (1, 0):
+                means = keep.tile([P, groups], F32, name="means%d_%d" % (i, h))
+                nc.scalar.activation(means[:], sums[h][:], COPY, scale=1.0 / GROUP)
+                nc.gpsimd.tensor_tensor(
+                    by_group(woven[z][h][:, :, t]),
+                    by_group(picked[i][:, h * HALF : (h + 1) * HALF]),
+                    spread(means),
+                    SUBTRACT,
+                )
+            if i == PACK + 1:
+                quantize(0, "window%d" % i)
+                multiply(0)
+        z, t = planes[last]
+        sums = gather_and_sum(last, (0, 1), ["sums_last", "means%d_1" % (last - 1)])
+        diff = work.tile([P, HALF], BF16, name="diff")
+        subtract(last, 0, sums, diff[:])
+        nc.scalar.copy(out=woven[z][0][:, :, t], in_=diff[:])
+        subtract(last, 1, sums, woven[z][1][:, :, t])
+        quantize(z, "codes_last")
+        multiply(z)
 
         for m in range(K_TILES):
             result = keep.tile([P, J], F32, name="result%d" % m)

@@ -22,11 +22,13 @@ AXIS_X = mybir.AxisListType.X
 
 P = 128
 PACK = 4
+PAIR = 2
 PASS_ROWS = P * PACK
 PASSES = N // PASS_ROWS
 GROUP = 8
 HALVES = 2
 HALF = J // HALVES
+HALF_GROUPS = HALF // GROUP
 LIST_ROWS = 16
 K_TILES = K // P
 
@@ -34,11 +36,11 @@ K_TILES = K // P
 def tile_list_group_relative_grad_kernel(tc, g, w_words, w_scales, rw, offs, out):
     nc = tc.nc
     planes = [(0, 0), (0, 1), (0, 2), (0, 3), (1, 2), (1, 0), (1, 1), (1, 3)]
+    last = len(planes) - 1
     g_planes = g.rearrange("(z p t) c -> z t p c", z=PASSES, t=PACK)
 
     with ExitStack() as ctx:
         keep = ctx.enter_context(tc.tile_pool(name="keep", bufs=1))
-        work = ctx.enter_context(tc.tile_pool(name="work", bufs=3))
         psum = ctx.enter_context(tc.psum_pool(name="psum", bufs=1))
 
         offsets = keep.tile([P, J // LIST_ROWS], U16, name="offsets")
@@ -71,16 +73,52 @@ def tile_list_group_relative_grad_kernel(tc, g, w_words, w_scales, rw, offs, out
             in_=rw_bank[:].rearrange("p c n -> p n c"),
         )
 
+        woven_first = keep.tile([P, J, PACK], BF16, name="woven0", align_bytes=64)
         woven = [
-            [keep.tile([P, HALF, PACK], BF16, name="woven%d_%d" % (z, h), align_bytes=64) for h in range(HALVES)]
-            for z in range(PASSES)
+            [woven_first[:, h * HALF : (h + 1) * HALF, :] for h in range(HALVES)],
+            [keep.tile([P, HALF, PACK], BF16, name="woven1_%d" % h, align_bytes=64)[:] for h in range(HALVES)],
         ]
+        picked = [keep.tile([P, J], F32, name="picked%d" % i) for i in range(len(planes))]
         codes = {}
         dscales = [keep.tile([P, J], U8, name="dscales%d" % z, align_bytes=64) for z in range(PASSES)]
         banks = [psum.tile([P, J], F32, name="bank%d" % m) for m in range(K_TILES)]
 
         def by_group(ap):
             return ap.rearrange("p (b i) -> p b i", i=GROUP)
+
+        def spread(tile):
+            return tile.unsqueeze(2).to_broadcast([P, HALF_GROUPS, GROUP])
+
+        def half(tile, h):
+            return tile[:, h * HALF : (h + 1) * HALF]
+
+        def gather_and_sum(i, order, sums):
+            cols = HALF // LIST_ROWS
+            for h in order:
+                nc.vector.tensor_copy(half(picked[i], h), windows[i][:].indirect(offsets[:, h * cols : (h + 1) * cols]))
+            for h in order:
+                nc.vector.tensor_reduce(sums[h], by_group(half(picked[i], h)), AXIS_X, ADD)
+
+        def small(name, tag=None):
+            tile = keep.tile([P, HALF_GROUPS], F32, name=name, tag=tag or name)
+            return tile[:]
+
+        def subtract(h, sums, target):
+            nc.vector.scalar_tensor_tensor(
+                out=by_group(target),
+                in0=spread(sums[h]),
+                scalar=-1.0 / GROUP,
+                in1=by_group(half(picked[last], h)),
+                op0=MULT,
+                op1=ADD,
+            )
+
+        def quantize(z, h):
+            nc.vector.quantize_mx(
+                out=half(codes[z], h).bitcast(E5M2X4),
+                scales=half(dscales[z], h),
+                in_=woven[z][h].rearrange("p j t -> p (j t)"),
+            )
 
         def multiply(z):
             for m in range(K_TILES):
@@ -94,66 +132,34 @@ def tile_list_group_relative_grad_kernel(tc, g, w_words, w_scales, rw, offs, out
                     stop=(z == PASSES - 1),
                 )
 
-        picked = [keep.tile([P, J], F32, name="picked%d" % i) for i in range(len(planes))]
-        groups = HALF // GROUP
-
-        def spread(tile):
-            return tile[:].unsqueeze(2).to_broadcast([P, groups, GROUP])
-
-        def gather_and_sum(i, order, tags):
-            sums = {}
-            for h in order:
-                lo, hi = h * HALF, (h + 1) * HALF
-                nc.vector.tensor_copy(
-                    picked[i][:, lo:hi], windows[i][:].indirect(offsets[:, lo // LIST_ROWS : hi // LIST_ROWS])
-                )
-            for h in order:
-                sums[h] = keep.tile([P, groups], F32, name="sums%d_%d" % (i, h), tag=tags[h])
-                nc.vector.tensor_reduce(sums[h][:], by_group(picked[i][:, h * HALF : (h + 1) * HALF]), AXIS_X, ADD)
-            return sums
-
-        def subtract(i, h, sums, target):
-            nc.vector.scalar_tensor_tensor(
-                out=by_group(target),
-                in0=spread(sums[h]),
-                scalar=-1.0 / GROUP,
-                in1=by_group(picked[i][:, h * HALF : (h + 1) * HALF]),
-                op0=MULT,
-                op1=ADD,
-            )
-
-        def quantize(z, tag):
-            codes[z] = keep.tile([P, J], U32, name="codes%d" % z, tag=tag, align_bytes=64)
-            for h in range(HALVES):
-                nc.vector.quantize_mx(
-                    out=codes[z][:, h * HALF : (h + 1) * HALF].bitcast(E5M2X4),
-                    scales=dscales[z][:, h * HALF : (h + 1) * HALF],
-                    in_=woven[z][h][:].rearrange("p j t -> p (j t)"),
-                )
-
-        last = len(planes) - 1
         for i in range(last):
             z, t = planes[i]
-            sums = gather_and_sum(i, (1, 0), ["sums%d_%d" % (i, h) for h in range(HALVES)])
+            sums = [small("sums%d_%d" % (i, h)) for h in range(HALVES)]
+            gather_and_sum(i, (1, 0), sums)
             for h in (1, 0):
-                means = keep.tile([P, groups], F32, name="means%d_%d" % (i, h))
-                nc.scalar.activation(means[:], sums[h][:], COPY, scale=1.0 / GROUP)
+                means = small("means%d_%d" % (i, h))
+                nc.scalar.activation(means, sums[h], COPY, scale=1.0 / GROUP)
                 nc.gpsimd.tensor_tensor(
-                    by_group(woven[z][h][:, :, t]),
-                    by_group(picked[i][:, h * HALF : (h + 1) * HALF]),
-                    spread(means),
-                    SUBTRACT,
+                    by_group(woven[z][h][:, :, t]), by_group(half(picked[i], h)), spread(means), SUBTRACT
                 )
             if i == PACK + 1:
-                quantize(0, "window%d" % i)
+                codes[0] = keep.tile([P, J], U32, name="codes0", tag="window%d" % i, align_bytes=64)
+                nc.vector.quantize_mx(
+                    out=codes[0][:].bitcast(E5M2X4),
+                    scales=dscales[0][:],
+                    in_=woven_first[:].rearrange("p j t -> p (j t)"),
+                )
                 multiply(0)
         z, t = planes[last]
-        sums = gather_and_sum(last, (0, 1), ["sums_last", "means%d_1" % (last - 1)])
-        diff = work.tile([P, HALF], BF16, name="diff")
-        subtract(last, 0, sums, diff[:])
+        sums = [small("sums_last"), small("sums_held", "means%d_1" % (last - 1))]
+        gather_and_sum(last, (0, 1), sums)
+        diff = keep.tile([P, HALF], BF16, name="diff")
+        subtract(0, sums, diff[:])
         nc.scalar.copy(out=woven[z][0][:, :, t], in_=diff[:])
-        subtract(last, 1, sums, woven[z][1][:, :, t])
-        quantize(z, "codes_last")
+        subtract(1, sums, woven[z][1][:, :, t])
+        codes[z] = keep.tile([P, J], U32, name="codes1", align_bytes=64)
+        for h in range(HALVES):
+            quantize(z, h)
         multiply(z)
 
         for m in range(K_TILES):

@@ -73,11 +73,7 @@ def tile_list_group_relative_grad_kernel(tc, g, w_words, w_scales, rw, offs, out
             in_=rw_bank[:].rearrange("p c n -> p n c"),
         )
 
-        woven_first = keep.tile([P, J, PACK], BF16, name="woven0", align_bytes=64)
-        woven = [
-            [woven_first[:, h * HALF : (h + 1) * HALF, :] for h in range(HALVES)],
-            [keep.tile([P, HALF, PACK], BF16, name="woven1_%d" % h, align_bytes=64)[:] for h in range(HALVES)],
-        ]
+        woven = [keep.tile([P, J, PACK], BF16, name="woven%d" % z, align_bytes=64) for z in range(PASSES)]
         picked = [keep.tile([P, J], F32, name="picked%d" % i) for i in range(len(planes))]
         codes = {}
         dscales = [keep.tile([P, J], U8, name="dscales%d" % z, align_bytes=64) for z in range(PASSES)]
@@ -103,21 +99,24 @@ def tile_list_group_relative_grad_kernel(tc, g, w_words, w_scales, rw, offs, out
             tile = keep.tile([P, HALF_GROUPS], F32, name=name, tag=tag or name)
             return tile[:]
 
-        def subtract(h, sums, target):
+        def subtract(lo, hi, sums, target):
+            h, first = divmod(lo, HALF)
+            groups = (hi - lo) // GROUP
+            part = sums[h][:, first // GROUP : first // GROUP + groups]
             nc.vector.scalar_tensor_tensor(
                 out=by_group(target),
-                in0=spread(sums[h]),
+                in0=part.unsqueeze(2).to_broadcast([P, groups, GROUP]),
                 scalar=-1.0 / GROUP,
-                in1=by_group(half(picked[last], h)),
+                in1=by_group(picked[last][:, lo:hi]),
                 op0=MULT,
                 op1=ADD,
             )
 
-        def quantize(z, h):
+        def quantize(z, lo, hi):
             nc.vector.quantize_mx(
-                out=half(codes[z], h).bitcast(E5M2X4),
-                scales=half(dscales[z], h),
-                in_=woven[z][h].rearrange("p j t -> p (j t)"),
+                out=codes[z][:, lo:hi].bitcast(E5M2X4),
+                scales=dscales[z][:, lo:hi],
+                in_=woven[z][:, lo:hi, :].rearrange("p j t -> p (j t)"),
             )
 
         def multiply(z):
@@ -140,29 +139,28 @@ def tile_list_group_relative_grad_kernel(tc, g, w_words, w_scales, rw, offs, out
                 means = small("means%d_%d" % (i, h))
                 nc.scalar.activation(means, sums[h], COPY, scale=1.0 / GROUP)
                 nc.gpsimd.tensor_tensor(
-                    by_group(woven[z][h][:, :, t]), by_group(half(picked[i], h)), spread(means), SUBTRACT
+                    by_group(woven[z][:, h * HALF : (h + 1) * HALF, t]), by_group(half(picked[i], h)), spread(means), SUBTRACT
                 )
             if i == PACK + 1:
                 codes[0] = keep.tile([P, J], U32, name="codes0", tag="window%d" % i, align_bytes=64)
-                nc.vector.quantize_mx(
-                    out=codes[0][:].bitcast(E5M2X4),
-                    scales=dscales[0][:],
-                    in_=woven_first[:].rearrange("p j t -> p (j t)"),
-                )
+                quantize(0, 0, J)
                 multiply(0)
         z, t = planes[last]
         sums = [small("sums_last"), small("sums_held", "means%d_1" % (last - 1))]
         gather_and_sum(last, (0, 1), sums)
-        diff = keep.tile([P, HALF], BF16, name="diff")
-        subtract(0, sums, diff[:])
-        nc.scalar.copy(out=woven[z][0][:, :, t], in_=diff[:])
-        subtract(1, sums, woven[z][1][:, :, t])
+        for lo, hi in ((0, 128), (128, 256), (256, 320)):
+            diff = keep.tile([P, hi - lo], BF16, name="diff%d" % lo)
+            subtract(lo, hi, sums, diff[:])
+            nc.scalar.copy(out=woven[z][:, lo:hi, t], in_=diff[:])
+        subtract(320, J, sums, woven[z][:, 320:J, t])
         codes[z] = keep.tile([P, J], U32, name="codes1", align_bytes=64)
-        for h in range(HALVES):
-            quantize(z, h)
+        for lo, hi in ((0, 128), (384, 512), (128, 384)):
+            quantize(z, lo, hi)
         multiply(z)
 
         for m in range(K_TILES):
-            result = keep.tile([P, J], F32, name="result%d" % m)
-            nc.vector.tensor_tensor(result[:], banks[m][:], rw_all[:], MULT)
-            nc.sync.dma_start(out=out[P * m : P * (m + 1), :], in_=result[:])
+            pieces = {0: [(0, P), (P, J)], K_TILES - 1: [(0, J - P), (J - P, J)]}.get(m, [(0, J)])
+            for lo, hi in pieces:
+                result = keep.tile([P, hi - lo], F32, name="result%d_%d" % (m, lo))
+                nc.vector.tensor_tensor(result[:], banks[m][:, lo:hi], rw_all[:, lo:hi], MULT)
+                nc.sync.dma_start(out=out[P * m : P * (m + 1), lo:hi], in_=result[:])

from contextlib import ExitStack

import concourse.mybir as mybir
from concourse.masks import make_identity

N, K, T, J = 1024, 512, 2048, 512
FLOPS = 2 * N * K * J

F32 = mybir.dt.float32
BF16 = mybir.dt.bfloat16
I32 = mybir.dt.int32
U32 = mybir.dt.uint32
U16 = mybir.dt.uint16
U8 = mybir.dt.uint8
E5M2X4 = mybir.dt.float8_e5m2_x4
E2M1X4 = mybir.dt.float4_e2m1fn_x4
ADD = mybir.AluOpType.add
MULT = mybir.AluOpType.mult
SUBTRACT = mybir.AluOpType.subtract
COPY = mybir.ActivationFunctionType.Copy
AXIS_X = mybir.AxisListType.X

P = 128
PACK = 4
PAIR = 2
PASS_ROWS = P * PACK
PASSES = N // PASS_ROWS
GROUP = 8
HALVES = 2
HALF = J // HALVES
HALF_GROUPS = HALF // GROUP
LIST_ROWS = 16
K_TILES = K // P


def tile_list_group_relative_grad_kernel(tc, g, w_words, w_scales, rw, offs, out):
    nc = tc.nc
    planes = [(0, 0), (0, 1), (0, 2), (0, 3), (1, 2), (1, 0), (1, 1), (1, 3)]
    last = len(planes) - 1
    g_planes = g.rearrange("(z p t) c -> z t p c", z=PASSES, t=PACK)

    with ExitStack() as ctx:
        keep = ctx.enter_context(tc.tile_pool(name="keep", bufs=1))
        psum = ctx.enter_context(tc.psum_pool(name="psum", bufs=1))

        offsets = keep.tile([P, J // LIST_ROWS], U16, name="offsets")
        windows = [keep.tile([P, T], F32, name="window%d" % i, align_bytes=64) for i in range(len(planes))]
        words = keep.tile([P, PASSES, 2 * K], U8, name="words", align_bytes=64)
        wscales = keep.tile([P, PASSES, K], U8, name="wscales", align_bytes=64)
        rw_rows = keep.tile([P, J // P], F32, name="rw_rows")
        rw_all = keep.tile([P, J], F32, name="rw_all")
        ident = keep.tile([P, P], F32, name="ident")

        nc.vector.memset(wscales[:].rearrange("p z c -> p (z c)").bitcast(I32), 0)
        nc.scalar.dma_start(out=rw_rows[:], in_=rw.rearrange("o (p c) -> (o p) c", p=P))
        for i, (z, t) in enumerate(planes):
            nc.sync.dma_start(out=windows[i][:], in_=g_planes[z, t])
            if i == 0:
                nc.sync.dma_start(offsets[:], offs)
        for q in range(4):
            nc.sync.dma_start(
                out=wscales[32 * q : 32 * q + 4].bitcast(I32),
                in_=w_scales[:, 4 * q : 4 * q + 4, :].rearrange("z r c -> r z c").bitcast(I32),
            )
        nc.sync.dma_start(out=words[:].bitcast(I32), in_=w_words.rearrange("z p c -> p z c").bitcast(I32))

        make_identity(nc, ident[:])
        rw_bank = psum.tile([P, J // P, P], F32, name="rw_bank")
        for c in range(J // P):
            nc.tensor.transpose(rw_bank[:, c, :], rw_rows[:, c : c + 1].to_broadcast([P, P]), ident[:])
        nc.scalar.copy(
            out=rw_all[:].rearrange("p (n c) -> p n c", c=J // P),
            in_=rw_bank[:].rearrange("p c n -> p n c"),
        )

        woven = [keep.tile([P, J, PACK], BF16, name="woven%d" % z, align_bytes=64) for z in range(PASSES)]
        picked = [keep.tile([P, J], F32, name="picked%d" % i) for i in range(len(planes))]
        codes = {}
        dscales = [keep.tile([P, J], U8, name="dscales%d" % z, align_bytes=64) for z in range(PASSES)]
        banks = [psum.tile([P, J], F32, name="bank%d" % m) for m in range(K_TILES)]

        def by_group(ap):
            return ap.rearrange("p (b i) -> p b i", i=GROUP)

        def spread(tile):
            return tile.unsqueeze(2).to_broadcast([P, HALF_GROUPS, GROUP])

        def half(tile, h):
            return tile[:, h * HALF : (h + 1) * HALF]

        def gather_and_sum(i, order, sums):
            cols = HALF // LIST_ROWS
            for h in order:
                nc.vector.tensor_copy(half(picked[i], h), windows[i][:].indirect(offsets[:, h * cols : (h + 1) * cols]))
            for h in order:
                nc.vector.tensor_reduce(sums[h], by_group(half(picked[i], h)), AXIS_X, ADD)

        def small(name, tag=None):
            tile = keep.tile([P, HALF_GROUPS], F32, name=name, tag=tag or name)
            return tile[:]

        def subtract(lo, hi, sums, target):
            h, first = divmod(lo, HALF)
            groups = (hi - lo) // GROUP
            part = sums[h][:, first // GROUP : first // GROUP + groups]
            nc.vector.scalar_tensor_tensor(
                out=by_group(target),
                in0=part.unsqueeze(2).to_broadcast([P, groups, GROUP]),
                scalar=-1.0 / GROUP,
                in1=by_group(picked[last][:, lo:hi]),
                op0=MULT,
                op1=ADD,
            )

        def quantize(z, lo, hi):
            nc.vector.quantize_mx(
                out=codes[z][:, lo:hi].bitcast(E5M2X4),
                scales=dscales[z][:, lo:hi],
                in_=woven[z][:, lo:hi, :].rearrange("p j t -> p (j t)"),
            )

        def multiply(z):
            for m in range(K_TILES):
                nc.tensor.matmul_mx(
                    out=banks[m][:],
                    lhsT=words[:, z, 2 * P * m : 2 * P * (m + 1)].bitcast(E2M1X4),
                    lhsT_scale=wscales[:, z, P * m : P * (m + 1)],
                    rhs=codes[z][:].bitcast(E5M2X4),
                    rhs_scale=dscales[z][:],
                    start=(z == 0),
                    stop=(z == PASSES - 1),
                )

        for i in range(last):
            z, t = planes[i]
            sums = [small("sums%d_%d" % (i, h)) for h in range(HALVES)]
            gather_and_sum(i, (1, 0), sums)
            for h in (1, 0):
                means = small("means%d_%d" % (i, h))
                nc.scalar.activation(means, sums[h], COPY, scale=1.0 / GROUP)
                nc.gpsimd.tensor_tensor(
                    by_group(woven[z][:, h * HALF : (h + 1) * HALF, t]), by_group(half(picked[i], h)), spread(means), SUBTRACT
                )
            if i == PACK + 1:
                codes[0] = keep.tile([P, J], U32, name="codes0", tag="window%d" % i, align_bytes=64)
                quantize(0, 0, J)
                multiply(0)
        z, t = planes[last]
        sums = [small("sums_last"), small("sums_held", "means%d_1" % (last - 1))]
        gather_and_sum(last, (0, 1), sums)
        for lo, hi in ((0, 128), (128, 256), (256, 320)):
            diff = keep.tile([P, hi - lo], BF16, name="diff%d" % lo)
            subtract(lo, hi, sums, diff[:])
            nc.scalar.copy(out=woven[z][:, lo:hi, t], in_=diff[:])
        subtract(320, J, sums, woven[z][:, 320:J, t])
        codes[z] = keep.tile([P, J], U32, name="codes1", align_bytes=64)
        for lo, hi in ((0, 128), (384, 512), (128, 384)):
            quantize(z, lo, hi)
        multiply(z)

        for m in range(K_TILES):
            pieces = {0: [(0, P), (P, J)], K_TILES - 1: [(0, J - P), (J - P, J)]}.get(m, [(0, J)])
            for lo, hi in pieces:
                result = keep.tile([P, hi - lo], F32, name="result%d_%d" % (m, lo))
                nc.vector.tensor_tensor(result[:], banks[m][:, lo:hi], rw_all[:, lo:hi], MULT)
                nc.sync.dma_start(out=out[P * m : P * (m + 1), lo:hi], in_=result[:])
